import numpy as np
import ml_dtypes

BF16 = ml_dtypes.bfloat16


def bf(x):
    return np.asarray(x, np.float32).astype(BF16)


def f32(x):
    return np.asarray(x, np.float32)


def f64(x):
    return np.asarray(x).astype(np.float64)


def striped(idx):
    return np.tile(idx.reshape(-1, 16).T, (8, 1))


S, K, M, N, D, V = 1024, 256, 256, 2048, 2, 1024


def setup_inputs():
    return {"table": bf(np.random.standard_normal((K, S))), "w": bf(np.random.standard_normal((D, K, M)) / np.sqrt(D * K)), "r": f32(np.random.standard_normal((M, V))), "offs": striped(np.random.permutation(np.tile(np.arange(S), 2))[:N])}


def reference(table, w, r, offs):
    idx = offs[:16].T.reshape(-1)
    x = f64(table)[:, idx]
    y = sum(f64(w)[t].T @ x[:, t * V : (t + 1) * V] for t in range(D))
    return y + f64(r)

@@ -1,0 +1,53 @@
+import concourse.mybir as mybir
+
+BF16, F32, U16 = mybir.dt.bfloat16, mybir.dt.float32, mybir.dt.uint16
+ADD = mybir.AluOpType.add
+
+P = 128
+NODES = 1024
+K = 256
+M = 256
+EDGES = 1024
+ENDS = 2
+PIECE = 512
+K_BLOCKS, M_BLOCKS, PIECES = K // P, M // P, EDGES // PIECE
+LIST_COLUMNS = PIECE // 16
+
+FLOPS = 2 * ENDS * K * M * EDGES
+
+
+def tile_gather_matmul_kernel(tc, table, w, r, offs, out):
+    nc = tc.nc
+    with (
+        tc.tile_pool(name="held", bufs=1) as held,
+        tc.tile_pool(name="results", bufs=M_BLOCKS * PIECES) as results,
+        tc.psum_pool(name="psum", bufs=M_BLOCKS * PIECES) as psum,
+    ):
+        offsets = held.tile([P, ENDS * EDGES // 16], U16, name="offsets")
+        nc.sync.dma_start(offsets[:], offs)
+        table_blocks = [held.tile([P, NODES], BF16, name=f"table{a}") for a in range(K_BLOCKS)]
+        for a in range(K_BLOCKS):
+            nc.sync.dma_start(table_blocks[a][:], table[a * P : (a + 1) * P, :])
+        weights = held.tile([P, ENDS * K_BLOCKS, M], BF16, name="weights")
+        nc.scalar.dma_start(weights[:], w.rearrange("t (a p) m -> p (t a) m", p=P))
+        r_blocks = [held.tile([P, EDGES], F32, name=f"r{b}") for b in range(M_BLOCKS)]
+        for b in range(M_BLOCKS):
+            nc.scalar.dma_start(r_blocks[b][:], r[b * P : (b + 1) * P, :])
+
+        for b in range(M_BLOCKS):
+            for c in range(PIECES):
+                terms = [(t, a) for t in range(ENDS) for a in range(K_BLOCKS)]
+                bank = psum.tile([P, PIECE], F32, name="bank")
+                for i, (t, a) in enumerate(terms):
+                    first = (t * PIECES + c) * LIST_COLUMNS
+                    nc.tensor.matmul(
+                        bank[:],
+                        weights[:, t * K_BLOCKS + a, b * P : (b + 1) * P],
+                        table_blocks[a][:].indirect(offsets[:, first : first + LIST_COLUMNS]),
+                        start=(i == 0),
+                        stop=(i == len(terms) - 1),
+                    )
+                edges = slice(c * PIECE, (c + 1) * PIECE)
+                result = results.tile([P, PIECE], F32, name="result")
+                nc.vector.tensor_tensor(result[:], bank[:], r_blocks[b][:, edges], ADD)
+                nc.sync.dma_start(out[b * P : (b + 1) * P, edges], result[:])

@@ -13,6 +13,8 @@ PIECE = 512
 K_BLOCKS, M_BLOCKS, PIECES = K // P, M // P, EDGES // PIECE
 LIST_COLUMNS = PIECE // 16
 
+WARM_UPS = 5
+
 FLOPS = 2 * ENDS * K * M * EDGES
 
 
@@ -21,7 +23,7 @@ def tile_gather_matmul_kernel(tc, table, w, r, offs, out):
     with (
         tc.tile_pool(name="held", bufs=1) as held,
         tc.tile_pool(name="results", bufs=M_BLOCKS * PIECES) as results,
-        tc.psum_pool(name="psum", bufs=M_BLOCKS * PIECES) as psum,
+        tc.psum_pool(name="psum", bufs=1) as psum,
     ):
         offsets = held.tile([P, ENDS * EDGES // 16], U16, name="offsets")
         nc.sync.dma_start(offsets[:], offs)
@@ -34,10 +36,16 @@ def tile_gather_matmul_kernel(tc, table, w, r, offs, out):
         for b in range(M_BLOCKS):
             nc.scalar.dma_start(r_blocks[b][:], r[b * P : (b + 1) * P, :])
 
+        zeros = held.tile([P, PIECE], BF16, name="zeros")
+        nc.vector.memset(zeros[:], 0.0)
+        unused = psum.tile([P, PIECE], F32, name="unused")
+        for i in range(WARM_UPS):
+            nc.tensor.matmul(unused[:], zeros[:, 0:P], zeros[:], start=True, stop=True)
+
         for b in range(M_BLOCKS):
             for c in range(PIECES):
                 terms = [(t, a) for t in range(ENDS) for a in range(K_BLOCKS)]
-                bank = psum.tile([P, PIECE], F32, name="bank")
+                bank = psum.tile([P, PIECE], F32, name=f"bank{b}{c}")
                 for i, (t, a) in enumerate(terms):
                     first = (t * PIECES + c) * LIST_COLUMNS
                     nc.tensor.matmul(

@@ -10,52 +10,49 @@ M = 256
 EDGES = 1024
 ENDS = 2
 PIECE = 512
+HALF = PIECE // 2
 K_BLOCKS, M_BLOCKS, PIECES = K // P, M // P, EDGES // PIECE
 LIST_COLUMNS = PIECE // 16
-
-WARM_UPS = 5
 
 FLOPS = 2 * ENDS * K * M * EDGES
 
 
 def tile_gather_matmul_kernel(tc, table, w, r, offs, out):
     nc = tc.nc
+    out_tiles = [(b, c) for b in range(M_BLOCKS) for c in range(PIECES)]
     with (
         tc.tile_pool(name="held", bufs=1) as held,
-        tc.tile_pool(name="results", bufs=M_BLOCKS * PIECES) as results,
+        tc.tile_pool(name="results", bufs=4) as results,
         tc.psum_pool(name="psum", bufs=1) as psum,
     ):
         offsets = held.tile([P, ENDS * EDGES // 16], U16, name="offsets")
         nc.sync.dma_start(offsets[:], offs)
         table_blocks = [held.tile([P, NODES], BF16, name=f"table{a}") for a in range(K_BLOCKS)]
+        weight_blocks = [held.tile([P, ENDS, M], BF16, name=f"weights{a}") for a in range(K_BLOCKS)]
         for a in range(K_BLOCKS):
-            nc.sync.dma_start(table_blocks[a][:], table[a * P : (a + 1) * P, :])
-        weights = held.tile([P, ENDS * K_BLOCKS, M], BF16, name="weights")
-        nc.scalar.dma_start(weights[:], w.rearrange("t (a p) m -> p (t a) m", p=P))
-        r_blocks = [held.tile([P, EDGES], F32, name=f"r{b}") for b in range(M_BLOCKS)]
-        for b in range(M_BLOCKS):
-            nc.scalar.dma_start(r_blocks[b][:], r[b * P : (b + 1) * P, :])
+            features = slice(a * P, (a + 1) * P)
+            nc.sync.dma_start(weight_blocks[a][:], w[:, features, :].rearrange("t p m -> p t m"))
+            nc.sync.dma_start(table_blocks[a][:], table[features, :])
+        r_tiles = {}
+        for b, c in out_tiles:
+            r_tiles[b, c] = held.tile([P, PIECE], F32, name=f"r{b}{c}")
+            nc.sync.dma_start(r_tiles[b, c][:], r[b * P : (b + 1) * P, c * PIECE : (c + 1) * PIECE])
 
-        zeros = held.tile([P, PIECE], BF16, name="zeros")
-        nc.vector.memset(zeros[:], 0.0)
-        unused = psum.tile([P, PIECE], F32, name="unused")
-        for i in range(WARM_UPS):
-            nc.tensor.matmul(unused[:], zeros[:, 0:P], zeros[:], start=True, stop=True)
-
-        for b in range(M_BLOCKS):
-            for c in range(PIECES):
-                terms = [(t, a) for t in range(ENDS) for a in range(K_BLOCKS)]
-                bank = psum.tile([P, PIECE], F32, name=f"bank{b}{c}")
-                for i, (t, a) in enumerate(terms):
-                    first = (t * PIECES + c) * LIST_COLUMNS
-                    nc.tensor.matmul(
-                        bank[:],
-                        weights[:, t * K_BLOCKS + a, b * P : (b + 1) * P],
-                        table_blocks[a][:].indirect(offsets[:, first : first + LIST_COLUMNS]),
-                        start=(i == 0),
-                        stop=(i == len(terms) - 1),
-                    )
-                edges = slice(c * PIECE, (c + 1) * PIECE)
-                result = results.tile([P, PIECE], F32, name="result")
-                nc.vector.tensor_tensor(result[:], bank[:], r_blocks[b][:, edges], ADD)
-                nc.sync.dma_start(out[b * P : (b + 1) * P, edges], result[:])
+        for b, c in out_tiles:
+            terms = [(a, t) for a in range(K_BLOCKS) for t in range(ENDS)]
+            bank = psum.tile([P, PIECE], F32, name=f"bank{b}{c}")
+            for i, (a, t) in enumerate(terms):
+                first = (t * PIECES + c) * LIST_COLUMNS
+                nc.tensor.matmul(
+                    bank[:],
+                    weight_blocks[a][:, t, b * P : (b + 1) * P],
+                    table_blocks[a][:].indirect(offsets[:, first : first + LIST_COLUMNS]),
+                    start=(i == 0),
+                    stop=(i == len(terms) - 1),
+                )
+            for h in range(PIECE // HALF):
+                columns = slice(h * HALF, (h + 1) * HALF)
+                result = results.tile([P, HALF], F32, name="result")
+                nc.vector.tensor_tensor(result[:], bank[:, columns], r_tiles[b, c][:, columns], ADD)
+                first_edge = c * PIECE + h * HALF
+                nc.scalar.dma_start(out[b * P : (b + 1) * P, first_edge : first_edge + HALF], result[:])

@@ -14,6 +14,8 @@ HALF = PIECE // 2
 K_BLOCKS, M_BLOCKS, PIECES = K // P, M // P, EDGES // PIECE
 LIST_COLUMNS = PIECE // 16
 
+WARM_UPS = 5
+
 FLOPS = 2 * ENDS * K * M * EDGES
 
 
@@ -37,6 +39,12 @@ def tile_gather_matmul_kernel(tc, table, w, r, offs, out):
         for b, c in out_tiles:
             r_tiles[b, c] = held.tile([P, PIECE], F32, name=f"r{b}{c}")
             nc.sync.dma_start(r_tiles[b, c][:], r[b * P : (b + 1) * P, c * PIECE : (c + 1) * PIECE])
+
+        zeros = held.tile([P, PIECE], BF16, name="zeros")
+        nc.vector.memset(zeros[:], 0.0)
+        unused = psum.tile([P, PIECE], F32, name="unused")
+        for i in range(WARM_UPS):
+            nc.tensor.matmul(unused[:], zeros[:, 0:P], zeros[:], start=True, stop=True)
 
         for b, c in out_tiles:
             terms = [(a, t) for a in range(K_BLOCKS) for t in range(ENDS)]

@@ -14,8 +14,6 @@ HALF = PIECE // 2
 K_BLOCKS, M_BLOCKS, PIECES = K // P, M // P, EDGES // PIECE
 LIST_COLUMNS = PIECE // 16
 
-WARM_UPS = 5
-
 FLOPS = 2 * ENDS * K * M * EDGES
 
 
@@ -30,21 +28,17 @@ def tile_gather_matmul_kernel(tc, table, w, r, offs, out):
         offsets = held.tile([P, ENDS * EDGES // 16], U16, name="offsets")
         nc.sync.dma_start(offsets[:], offs)
         table_blocks = [held.tile([P, NODES], BF16, name=f"table{a}") for a in range(K_BLOCKS)]
-        weight_blocks = [held.tile([P, ENDS, M], BF16, name=f"weights{a}") for a in range(K_BLOCKS)]
+        weight_tiles = {}
         for a in range(K_BLOCKS):
             features = slice(a * P, (a + 1) * P)
-            nc.sync.dma_start(weight_blocks[a][:], w[:, features, :].rearrange("t p m -> p t m"))
             nc.sync.dma_start(table_blocks[a][:], table[features, :])
+            for t in range(ENDS):
+                weight_tiles[a, t] = held.tile([P, M], BF16, name=f"weights{a}{t}")
+                nc.sync.dma_start(weight_tiles[a, t][:], w[t, features, :])
         r_tiles = {}
         for b, c in out_tiles:
             r_tiles[b, c] = held.tile([P, PIECE], F32, name=f"r{b}{c}")
             nc.sync.dma_start(r_tiles[b, c][:], r[b * P : (b + 1) * P, c * PIECE : (c + 1) * PIECE])
-
-        zeros = held.tile([P, PIECE], BF16, name="zeros")
-        nc.vector.memset(zeros[:], 0.0)
-        unused = psum.tile([P, PIECE], F32, name="unused")
-        for i in range(WARM_UPS):
-            nc.tensor.matmul(unused[:], zeros[:, 0:P], zeros[:], start=True, stop=True)
 
         for b, c in out_tiles:
             terms = [(a, t) for a in range(K_BLOCKS) for t in range(ENDS)]
@@ -53,7 +47,7 @@ def tile_gather_matmul_kernel(tc, table, w, r, offs, out):
                 first = (t * PIECES + c) * LIST_COLUMNS
                 nc.tensor.matmul(
                     bank[:],
-                    weight_blocks[a][:, t, b * P : (b + 1) * P],
+                    weight_tiles[a, t][:, b * P : (b + 1) * P],
                     table_blocks[a][:].indirect(offsets[:, first : first + LIST_COLUMNS]),
                     start=(i == 0),
                     stop=(i == len(terms) - 1),
@@ -63,4 +57,5 @@ def tile_gather_matmul_kernel(tc, table, w, r, offs, out):
                 result = results.tile([P, HALF], F32, name="result")
                 nc.vector.tensor_tensor(result[:], bank[:, columns], r_tiles[b, c][:, columns], ADD)
                 first_edge = c * PIECE + h * HALF
-                nc.scalar.dma_start(out[b * P : (b + 1) * P, first_edge : first_edge + HALF], result[:])
+                queue = (nc.scalar, nc.sync)[h]
+                queue.dma_start(out[b * P : (b + 1) * P, first_edge : first_edge + HALF], result[:])

@@ -22,7 +22,6 @@ def tile_gather_matmul_kernel(tc, table, w, r, offs, out):
     out_tiles = [(b, c) for b in range(M_BLOCKS) for c in range(PIECES)]
     with (
         tc.tile_pool(name="held", bufs=1) as held,
-        tc.tile_pool(name="results", bufs=4) as results,
         tc.psum_pool(name="psum", bufs=1) as psum,
     ):
         offsets = held.tile([P, ENDS * EDGES // 16], U16, name="offsets")
@@ -54,8 +53,8 @@ def tile_gather_matmul_kernel(tc, table, w, r, offs, out):
                 )
             for h in range(PIECE // HALF):
                 columns = slice(h * HALF, (h + 1) * HALF)
-                result = results.tile([P, HALF], F32, name="result")
-                nc.vector.tensor_tensor(result[:], bank[:, columns], r_tiles[b, c][:, columns], ADD)
+                result = r_tiles[b, c][:, columns]
+                nc.vector.tensor_tensor(result, bank[:, columns], result, ADD)
                 first_edge = c * PIECE + h * HALF
                 queue = (nc.scalar, nc.sync)[h]
-                queue.dma_start(out[b * P : (b + 1) * P, first_edge : first_edge + HALF], result[:])
+                queue.dma_start(out[b * P : (b + 1) * P, first_edge : first_edge + HALF], result)

@@ -56,5 +56,4 @@ def tile_gather_matmul_kernel(tc, table, w, r, offs, out):
                 result = r_tiles[b, c][:, columns]
                 nc.vector.tensor_tensor(result, bank[:, columns], result, ADD)
                 first_edge = c * PIECE + h * HALF
-                queue = (nc.scalar, nc.sync)[h]
-                queue.dma_start(out[b * P : (b + 1) * P, first_edge : first_edge + HALF], result)
+                nc.sync.dma_start(out[b * P : (b + 1) * P, first_edge : first_edge + HALF], result)

@@ -28,12 +28,14 @@ def tile_gather_matmul_kernel(tc, table, w, r, offs, out):
         nc.sync.dma_start(offsets[:], offs)
         table_blocks = [held.tile([P, NODES], BF16, name=f"table{a}") for a in range(K_BLOCKS)]
         weight_tiles = {}
-        for a in range(K_BLOCKS):
-            features = slice(a * P, (a + 1) * P)
-            nc.sync.dma_start(table_blocks[a][:], table[features, :])
-            for t in range(ENDS):
-                weight_tiles[a, t] = held.tile([P, M], BF16, name=f"weights{a}{t}")
-                nc.sync.dma_start(weight_tiles[a, t][:], w[t, features, :])
+        for b in range(M_BLOCKS):
+            for a in range(K_BLOCKS):
+                features = slice(a * P, (a + 1) * P)
+                if b == 0:
+                    nc.sync.dma_start(table_blocks[a][:], table[features, :])
+                for t in range(ENDS):
+                    weight_tiles[a, t, b] = held.tile([P, P], BF16, name=f"weights{a}{t}{b}")
+                    nc.sync.dma_start(weight_tiles[a, t, b][:], w[t, features, b * P : (b + 1) * P])
         r_tiles = {}
         for b, c in out_tiles:
             r_tiles[b, c] = held.tile([P, PIECE], F32, name=f"r{b}{c}")
@@ -46,7 +48,7 @@ def tile_gather_matmul_kernel(tc, table, w, r, offs, out):
                 first = (t * PIECES + c) * LIST_COLUMNS
                 nc.tensor.matmul(
                     bank[:],
-                    weight_tiles[a, t][:, b * P : (b + 1) * P],
+                    weight_tiles[a, t, b][:],
                     table_blocks[a][:].indirect(offsets[:, first : first + LIST_COLUMNS]),
                     start=(i == 0),
                     stop=(i == len(terms) - 1),

@@ -28,11 +28,10 @@ def tile_gather_matmul_kernel(tc, table, w, r, offs, out):
         nc.sync.dma_start(offsets[:], offs)
         table_blocks = [held.tile([P, NODES], BF16, name=f"table{a}") for a in range(K_BLOCKS)]
         weight_tiles = {}
-        for b in range(M_BLOCKS):
-            for a in range(K_BLOCKS):
-                features = slice(a * P, (a + 1) * P)
-                if b == 0:
-                    nc.sync.dma_start(table_blocks[a][:], table[features, :])
+        for a in range(K_BLOCKS):
+            features = slice(a * P, (a + 1) * P)
+            nc.sync.dma_start(table_blocks[a][:], table[features, :])
+            for b in range(M_BLOCKS):
                 for t in range(ENDS):
                     weight_tiles[a, t, b] = held.tile([P, P], BF16, name=f"weights{a}{t}{b}")
                     nc.sync.dma_start(weight_tiles[a, t, b][:], w[t, features, b * P : (b + 1) * P])

@@ -25,12 +25,13 @@ def tile_gather_matmul_kernel(tc, table, w, r, offs, out):
         tc.psum_pool(name="psum", bufs=1) as psum,
     ):
         offsets = held.tile([P, ENDS * EDGES // 16], U16, name="offsets")
-        nc.sync.dma_start(offsets[:], offs)
         table_blocks = [held.tile([P, NODES], BF16, name=f"table{a}") for a in range(K_BLOCKS)]
         weight_tiles = {}
         for a in range(K_BLOCKS):
             features = slice(a * P, (a + 1) * P)
             nc.sync.dma_start(table_blocks[a][:], table[features, :])
+            if a == 0:
+                nc.sync.dma_start(offsets[:], offs)
             for b in range(M_BLOCKS):
                 for t in range(ENDS):
                     weight_tiles[a, t, b] = held.tile([P, P], BF16, name=f"weights{a}{t}{b}")

@@ -27,15 +27,15 @@ def tile_gather_matmul_kernel(tc, table, w, r, offs, out):
         offsets = held.tile([P, ENDS * EDGES // 16], U16, name="offsets")
         table_blocks = [held.tile([P, NODES], BF16, name=f"table{a}") for a in range(K_BLOCKS)]
         weight_tiles = {}
+        nc.sync.dma_start(table_blocks[0][:], table[0:P, :])
+        nc.sync.dma_start(offsets[:], offs)
         for a in range(K_BLOCKS):
             features = slice(a * P, (a + 1) * P)
-            nc.sync.dma_start(table_blocks[a][:], table[features, :])
-            if a == 0:
-                nc.sync.dma_start(offsets[:], offs)
             for b in range(M_BLOCKS):
                 for t in range(ENDS):
                     weight_tiles[a, t, b] = held.tile([P, P], BF16, name=f"weights{a}{t}{b}")
                     nc.sync.dma_start(weight_tiles[a, t, b][:], w[t, features, b * P : (b + 1) * P])
+        nc.sync.dma_start(table_blocks[1][:], table[P : 2 * P, :])
         r_tiles = {}
         for b, c in out_tiles:
             r_tiles[b, c] = held.tile([P, PIECE], F32, name=f"r{b}{c}")

@@ -29,17 +29,23 @@ def tile_gather_matmul_kernel(tc, table, w, r, offs, out):
         weight_tiles = {}
         nc.sync.dma_start(table_blocks[0][:], table[0:P, :])
         nc.sync.dma_start(offsets[:], offs)
-        for a in range(K_BLOCKS):
-            features = slice(a * P, (a + 1) * P)
-            for b in range(M_BLOCKS):
-                for t in range(ENDS):
-                    weight_tiles[a, t, b] = held.tile([P, P], BF16, name=f"weights{a}{t}{b}")
-                    nc.sync.dma_start(weight_tiles[a, t, b][:], w[t, features, b * P : (b + 1) * P])
+        first_weights = held.tile([P, P], BF16, name="first_weights")
+        nc.sync.dma_start(first_weights[:], w[0, 0:P, 0:P])
+        target_weights = held.tile([P, M], BF16, name="target_weights")
+        nc.sync.dma_start(target_weights[:], w[1, 0:P, :])
+        source_weights = held.tile([P, P], BF16, name="source_weights")
+        nc.sync.dma_start(source_weights[:], w[0, 0:P, P:M])
         nc.sync.dma_start(table_blocks[1][:], table[P : 2 * P, :])
-        r_tiles = {}
-        for b, c in out_tiles:
-            r_tiles[b, c] = held.tile([P, PIECE], F32, name=f"r{b}{c}")
-            nc.sync.dma_start(r_tiles[b, c][:], r[b * P : (b + 1) * P, c * PIECE : (c + 1) * PIECE])
+        later_weights = held.tile([P, ENDS, M], BF16, name="later_weights")
+        nc.sync.dma_start(later_weights[:], w[:, P : 2 * P, :].rearrange("t k m -> k t m"))
+        weight_tiles[0, 0, 0] = first_weights[:]
+        weight_tiles[0, 0, 1] = source_weights[:]
+        for b in range(M_BLOCKS):
+            weight_tiles[0, 1, b] = target_weights[:, b * P : (b + 1) * P]
+            for t in range(ENDS):
+                weight_tiles[1, t, b] = later_weights[:, t, b * P : (b + 1) * P]
+        r_tile = held.tile([P, M_BLOCKS, EDGES], F32, name="r_tile")
+        nc.sync.dma_start(r_tile[:], r.rearrange("(b p) e -> p b e", p=P))
 
         for b, c in out_tiles:
             terms = [(a, t) for a in range(K_BLOCKS) for t in range(ENDS)]
@@ -48,14 +54,14 @@ def tile_gather_matmul_kernel(tc, table, w, r, offs, out):
                 first = (t * PIECES + c) * LIST_COLUMNS
                 nc.tensor.matmul(
                     bank[:],
-                    weight_tiles[a, t, b][:],
+                    weight_tiles[a, t, b],
                     table_blocks[a][:].indirect(offsets[:, first : first + LIST_COLUMNS]),
                     start=(i == 0),
                     stop=(i == len(terms) - 1),
                 )
             for h in range(PIECE // HALF):
                 columns = slice(h * HALF, (h + 1) * HALF)
-                result = r_tiles[b, c][:, columns]
-                nc.vector.tensor_tensor(result, bank[:, columns], result, ADD)
                 first_edge = c * PIECE + h * HALF
+                result = r_tile[:, b, first_edge : first_edge + HALF]
+                nc.vector.tensor_tensor(result, bank[:, columns], result, ADD)
                 nc.sync.dma_start(out[b * P : (b + 1) * P, first_edge : first_edge + HALF], result)

@@ -28,9 +28,9 @@ def tile_gather_matmul_kernel(tc, table, w, r, offs, out):
         table_blocks = [held.tile([P, NODES], BF16, name=f"table{a}") for a in range(K_BLOCKS)]
         weight_tiles = {}
         nc.sync.dma_start(table_blocks[0][:], table[0:P, :])
-        nc.sync.dma_start(offsets[:], offs)
         first_weights = held.tile([P, P], BF16, name="first_weights")
         nc.sync.dma_start(first_weights[:], w[0, 0:P, 0:P])
+        nc.sync.dma_start(offsets[:], offs)
         target_weights = held.tile([P, M], BF16, name="target_weights")
         nc.sync.dma_start(target_weights[:], w[1, 0:P, :])
         source_weights = held.tile([P, P], BF16, name="source_weights")

import concourse.mybir as mybir

BF16, F32, U16 = mybir.dt.bfloat16, mybir.dt.float32, mybir.dt.uint16
ADD = mybir.AluOpType.add

P = 128
NODES = 1024
K = 256
M = 256
EDGES = 1024
ENDS = 2
PIECE = 512
HALF = PIECE // 2
K_BLOCKS, M_BLOCKS, PIECES = K // P, M // P, EDGES // PIECE
LIST_COLUMNS = PIECE // 16

FLOPS = 2 * ENDS * K * M * EDGES


def tile_gather_matmul_kernel(tc, table, w, r, offs, out):
    nc = tc.nc
    out_tiles = [(b, c) for b in range(M_BLOCKS) for c in range(PIECES)]
    with (
        tc.tile_pool(name="held", bufs=1) as held,
        tc.psum_pool(name="psum", bufs=1) as psum,
    ):
        offsets = held.tile([P, ENDS * EDGES // 16], U16, name="offsets")
        table_blocks = [held.tile([P, NODES], BF16, name=f"table{a}") for a in range(K_BLOCKS)]
        weight_tiles = {}
        nc.sync.dma_start(table_blocks[0][:], table[0:P, :])
        first_weights = held.tile([P, P], BF16, name="first_weights")
        nc.sync.dma_start(first_weights[:], w[0, 0:P, 0:P])
        nc.sync.dma_start(offsets[:], offs)
        target_weights = held.tile([P, M], BF16, name="target_weights")
        nc.sync.dma_start(target_weights[:], w[1, 0:P, :])
        source_weights = held.tile([P, P], BF16, name="source_weights")
        nc.sync.dma_start(source_weights[:], w[0, 0:P, P:M])
        nc.sync.dma_start(table_blocks[1][:], table[P : 2 * P, :])
        later_weights = held.tile([P, ENDS, M], BF16, name="later_weights")
        nc.sync.dma_start(later_weights[:], w[:, P : 2 * P, :].rearrange("t k m -> k t m"))
        weight_tiles[0, 0, 0] = first_weights[:]
        weight_tiles[0, 0, 1] = source_weights[:]
        for b in range(M_BLOCKS):
            weight_tiles[0, 1, b] = target_weights[:, b * P : (b + 1) * P]
            for t in range(ENDS):
                weight_tiles[1, t, b] = later_weights[:, t, b * P : (b + 1) * P]
        r_tile = held.tile([P, M_BLOCKS, EDGES], F32, name="r_tile")
        nc.sync.dma_start(r_tile[:], r.rearrange("(b p) e -> p b e", p=P))

        for b, c in out_tiles:
            terms = [(a, t) for a in range(K_BLOCKS) for t in range(ENDS)]
            bank = psum.tile([P, PIECE], F32, name=f"bank{b}{c}")
            for i, (a, t) in enumerate(terms):
                first = (t * PIECES + c) * LIST_COLUMNS
                nc.tensor.matmul(
                    bank[:],
                    weight_tiles[a, t, b],
                    table_blocks[a][:].indirect(offsets[:, first : first + LIST_COLUMNS]),
                    start=(i == 0),
                    stop=(i == len(terms) - 1),
                )
            for h in range(PIECE // HALF):
                columns = slice(h * HALF, (h + 1) * HALF)
                first_edge = c * PIECE + h * HALF
                result = r_tile[:, b, first_edge : first_edge + HALF]
                nc.vector.tensor_tensor(result, bank[:, columns], result, ADD)
                nc.sync.dma_start(out[b * P : (b + 1) * P, first_edge : first_edge + HALF], result)
